import numpy as np
import ml_dtypes


def mxq(x, axis, fmt="e4m3"):
    dtype, down = {"e4m3": (ml_dtypes.float8_e4m3fn, 7), "e5m2": (ml_dtypes.float8_e5m2, 14)}[fmt]
    v = np.moveaxis(np.asarray(x, np.float32).astype(ml_dtypes.bfloat16).astype(np.float64), axis, -1)
    blocks = v.reshape(v.shape[:-1] + (-1, 32))
    amax = np.abs(blocks).max(-1, keepdims=True)
    byte = np.maximum(np.where(amax > 0, np.frexp(amax)[1] - 1 + 127, 0) - down, 1)
    scale = np.exp2(byte - 127.0)
    codes = (blocks / scale).astype(np.float32).astype(dtype).astype(np.float64)
    return np.moveaxis((codes * scale).reshape(v.shape), -1, axis)


WIDE = False


def mx_kscale(k):
    if not WIDE:
        return np.ones(k)
    levels = np.array([10, -10, 5, -5, 0])
    if k % 512:
        return np.exp2(np.random.permutation(np.resize(levels, k // 32))).repeat(32)
    a = np.empty((k // 512, 16))
    for p in range(k // 512):
        a[p, :8] = np.random.permutation(np.resize(levels, 8))
        for g in range(8):
            far = levels[np.abs(levels - a[p, g]) >= 10]
            a[p, g + 8] = far[np.random.randint(len(far))]
    return np.exp2(a.ravel()).repeat(32)


def f64(x):
    return np.asarray(x).astype(np.float64)


def striped8(idx):
    return np.asarray(idx).reshape(8, -1, 16).transpose(0, 2, 1).reshape(128, -1).astype(np.uint16)


def unstriped8(offs):
    return offs.reshape(8, 16, -1).transpose(0, 2, 1).reshape(8, -1).astype(np.int64)


def pick8(x, idx, run):
    r = np.arange(len(x))
    return x[r[:, None], idx[r % (8 * run) // run]]


E2M1 = np.array([0.0, 0.5, 1.0, 1.5, 2.0, 3.0, 4.0, 6.0, -0.0, -0.5, -1.0, -1.5, -2.0, -3.0, -4.0, -6.0])


def pack_weight(w, fmt):
    k, n = w.shape
    w = f64(np.asarray(w, np.float32).astype(ml_dtypes.bfloat16)).reshape(k // 32, 32, n)
    amax = np.abs(w).max(1)
    if fmt == "e4m3":
        byte = np.frexp(amax)[1] - 1 + 127 - 7
    else:
        mant, ex = np.frexp(amax / 6.0)
        byte = np.where(mant > 0.5, ex, ex - 1) + 127
    byte = np.clip(np.where(amax > 0, byte, 1), 1, 254)
    scaled = (w * np.exp2(127.0 - byte)[:, None, :]).reshape(k, n).astype(np.float32)
    by_word = np.ascontiguousarray(scaled.reshape(k // 512, 128, 4, n).transpose(0, 1, 3, 2))
    if fmt == "e4m3":
        words = by_word.astype(ml_dtypes.float8_e4m3fn).view(np.uint8)
    else:
        c = by_word.astype(ml_dtypes.float4_e2m1fn).view(np.uint8) & 0xF
        words = (c[..., 0::2] | (c[..., 1::2] << 4)).reshape(k // 512, 128, 2 * n)
    return np.ascontiguousarray(words), np.ascontiguousarray(byte.astype(np.uint8).reshape(k // 512, 16, n))


def unpack_weight(words, scales, fmt):
    g, _, n = scales.shape
    words = np.ascontiguousarray(words).reshape(g, 128, n, -1)
    if fmt == "e4m3":
        vals = words.view(ml_dtypes.float8_e4m3fn).astype(np.float64)
    else:
        nib = np.empty((g, 128, n, 4), np.uint8)
        nib[..., 0::2] = words & 0xF
        nib[..., 1::2] = words >> 4
        vals = E2M1[nib]
    vals = vals * np.repeat(np.exp2(scales.astype(np.float64) - 127.0), 8, axis=1)[..., None]
    return vals.transpose(0, 1, 3, 2).reshape(g * 512, n)


D, T, U, X, I, Q = 512, 1024, 1024, 1024, 512, 128


def setup_inputs():
    n = np.random.standard_normal
    idx = np.stack([np.random.permutation(T)[:I] for _ in range(8)])
    idx2 = np.stack([np.random.permutation(U)[:I] for _ in range(8)])
    idx3 = np.stack([np.random.permutation(X)[:I] for _ in range(8)])
    idx4 = np.stack([np.random.permutation(X)[:I] for _ in range(8)])
    fd = mx_kscale(D)
    keysp = pack_weight(n((D, T)) / fd[:, None], "e2m1")
    notesp = pack_weight(n((D, U)) / fd[:, None], "e4m3")
    usersp = pack_weight(n((D, X)) / fd[:, None], "e2m1")
    return {
        "query": (n((D, Q)) * 1.0 / np.sqrt(D) * fd[:, None]).astype(np.float32),
        "keys_words": keysp[0],
        "keys_scales": keysp[1],
        "notes_words": notesp[0],
        "notes_scales": notesp[1],
        "users_words": usersp[0],
        "users_scales": usersp[1],
        "lam": (np.random.uniform(0.5, 1.5, (Q, 1))).astype(np.float32),
        "offs": striped8(idx),
        "offs2": striped8(idx2),
        "offs3": striped8(idx3),
        "offs4": striped8(idx4),
    }


def reference(query, keys_words, keys_scales, notes_words, notes_scales, users_words, users_scales, lam, offs, offs2, offs3, offs4):
    idx = unstriped8(offs)
    idx2 = unstriped8(offs2)
    idx3 = unstriped8(offs3)
    idx4 = unstriped8(offs4)
    keysu = unpack_weight(keys_words, keys_scales, "e2m1")
    notesu = unpack_weight(notes_words, notes_scales, "e4m3")
    usersu = unpack_weight(users_words, users_scales, "e2m1")
    queryq = mxq(f64(query), 0, "e4m3")
    a = queryq.T @ keysu
    b = queryq.T @ notesu
    c0 = queryq.T @ usersu
    r = pick8(a, idx, 16) - pick8(b, idx2, 16)
    f1 = np.zeros((Q, X))
    f1[np.arange(Q)[:, None], idx3[np.arange(Q) % 128 // 16]] = r
    cc = c0 + f1 * f64(lam)
    y = pick8(cc, idx4, 16) - r
    return y

@@ -1,0 +1,157 @@
+from contextlib import ExitStack
+
+import concourse.mybir as mybir
+
+F32 = mybir.dt.float32
+BF16 = mybir.dt.bfloat16
+I32 = mybir.dt.int32
+U32 = mybir.dt.uint32
+U16 = mybir.dt.uint16
+U8 = mybir.dt.uint8
+FP8X4 = mybir.dt.float8_e4m3fn_x4
+FP4X4 = mybir.dt.float4_e2m1fn_x4
+COPY = mybir.ActivationFunctionType.Copy
+ADD = mybir.AluOpType.add
+SUB = mybir.AluOpType.subtract
+MULT = mybir.AluOpType.mult
+
+P = 128
+PACK = 4
+D, COLS, SLOTS, Q = 512, 1024, 512, 128
+BANK = 512
+HALF = SLOTS // 2
+LIST_COLS = SLOTS // 16
+CAST_SPLIT = 48
+
+FLOPS = 2 * Q * D * 3 * COLS
+
+
+def load_scale_rows(nc, plane, scales):
+    for quad in range(4):
+        nc.sync.dma_start(
+            out=plane[32 * quad : 32 * quad + 4, :].bitcast(I32),
+            in_=scales[0, 4 * quad : 4 * quad + 4, :].bitcast(I32),
+        )
+
+
+def tile_attend_tugged_three_kernel(tc, query, keys_words, keys_scales, notes_words, notes_scales,
+                                     users_words, users_scales, lam, offs, offs2, offs3, offs4, out):
+    nc = tc.nc
+    with ExitStack() as ctx:
+        lists = ctx.enter_context(tc.tile_pool(name="lists", bufs=1))
+        sb = ctx.enter_context(tc.tile_pool(name="sb", bufs=1))
+        ps = ctx.enter_context(tc.psum_pool(name="ps", bufs=1))
+
+        token_list = lists.tile([P, LIST_COLS], U16, name="token_list")
+        note_list = lists.tile([P, LIST_COLS], U16, name="note_list")
+        tug_list = lists.tile([P, LIST_COLS], U16, name="tug_list")
+        read_list = lists.tile([P, LIST_COLS], U16, name="read_list")
+
+        def half(lst, h):
+            return lst[:, h * (LIST_COLS // 2) : (h + 1) * (LIST_COLS // 2)]
+
+        q_raw = sb.tile([P, PACK, Q], F32, name="q_raw")
+        q_bf = sb.tile([P, Q, PACK], BF16, name="q_bf", align_bytes=64)
+        q_codes = sb.tile([P, Q], U32, name="q_codes", align_bytes=64)
+        q_scale = sb.tile([P, Q], U8, name="q_scale", align_bytes=64)
+        k_words = sb.tile([P, 2 * COLS], U8, name="k_words", align_bytes=64)
+        n_words = sb.tile([P, COLS], U32, name="n_words", tag="notes_then_a", align_bytes=64)
+        u_words = sb.tile([P, 2 * COLS], U8, name="u_words", align_bytes=64)
+        k_scale = sb.tile([P, COLS], U8, name="k_scale", align_bytes=64)
+        n_scale = sb.tile([P, COLS], U8, name="n_scale", align_bytes=64)
+        u_scale = sb.tile([P, COLS], U8, name="u_scale", align_bytes=64)
+        lam_sb = sb.tile([P, 1], F32, name="lam_sb")
+        a_sb = sb.tile([P, COLS], F32, name="a_sb")
+        b_sb = sb.tile([P, COLS], F32, name="b_sb")
+        f1 = sb.tile([P, COLS], F32, name="f1")
+        cc = sb.tile([P, COLS], F32, name="cc")
+
+        for plane in (k_scale, n_scale, u_scale):
+            nc.vector.memset(plane[:].bitcast(I32), 0)
+        nc.vector.memset(f1[:], 0.0)
+
+        nc.sync.dma_start(token_list[:], offs)
+        nc.sync.dma_start(out=q_raw[:], in_=query.rearrange("(p j) q -> p j q", j=PACK))
+        load_scale_rows(nc, k_scale, keys_scales)
+        nc.sync.dma_start(note_list[:], offs2)
+        nc.sync.dma_start(out=k_words[:].bitcast(I32), in_=keys_words[0].bitcast(I32))
+        nc.sync.dma_start(
+            out=n_words[:].bitcast(I32), in_=notes_words[0].rearrange("p n t -> p (n t)").bitcast(I32)
+        )
+        load_scale_rows(nc, n_scale, notes_scales)
+        nc.sync.dma_start(tug_list[:], offs3)
+        load_scale_rows(nc, u_scale, users_scales)
+        nc.sync.dma_start(out=u_words[:].bitcast(I32), in_=users_words[0].bitcast(I32))
+        nc.sync.dma_start(out=lam_sb[:], in_=lam)
+        nc.sync.dma_start(read_list[:], offs4)
+
+        q_src = q_raw[:].rearrange("p j q -> p q j")
+        nc.vector.tensor_copy(out=q_bf[:, :CAST_SPLIT, :], in_=q_src[:, :CAST_SPLIT, :])
+        nc.scalar.activation(q_bf[:, CAST_SPLIT:, :], q_src[:, CAST_SPLIT:, :], COPY)
+        nc.vector.quantize_mx(
+            out=q_codes[:].bitcast(FP8X4), scales=q_scale[:], in_=q_bf[:].rearrange("p q j -> p (q j)")
+        )
+
+        def scores(name, words, scale, first, width):
+            bank = ps.tile([Q, width], F32, name=name)
+            nc.tensor.matmul_mx(
+                out=bank[:],
+                lhsT=q_codes[:].bitcast(FP8X4),
+                lhsT_scale=q_scale[:],
+                rhs=words,
+                rhs_scale=scale[:, first : first + width],
+                start=True,
+                stop=True,
+            )
+            return bank
+
+        def fp4_scores(name, words, scale, first, width):
+            return scores(name, words[:, 2 * first : 2 * (first + width)].bitcast(FP4X4), scale, first, width)
+
+        def fp8_scores(name, words, scale, first, width):
+            return scores(name, words[:, first : first + width].bitcast(FP8X4), scale, first, width)
+
+        a0 = fp4_scores("a0", k_words, k_scale, 0, BANK)
+        a1 = fp4_scores("a1", k_words, k_scale, BANK, BANK)
+        b0 = fp8_scores("b0", n_words, n_scale, 0, BANK)
+        b1 = fp8_scores("b1", n_words, n_scale, BANK, BANK // 2)
+        b2 = fp8_scores("b2", n_words, n_scale, BANK + BANK // 2, BANK // 2)
+        c_banks = [fp4_scores("c%d" % h, u_words, u_scale, h * BANK, BANK) for h in range(2)]
+
+        nc.vector.tensor_copy(out=a_sb[:, :BANK], in_=a0[:])
+        nc.scalar.activation(a_sb[:, BANK:], a1[:], COPY)
+        a_first = sb.tile([P, HALF], F32, name="a_first")
+        nc.scalar.activation(a_first[:], a_sb[:].indirect(half(token_list, 0)), COPY)
+        nc.vector.tensor_copy(out=b_sb[:, :BANK], in_=b0[:])
+        nc.scalar.activation(b_sb[:, BANK : BANK + BANK // 2], b1[:], COPY)
+        nc.vector.tensor_copy(out=b_sb[:, BANK + BANK // 2 :], in_=b2[:])
+
+        a_second = sb.tile([P, HALF], F32, name="a_second", tag="notes_then_a", align_bytes=64)
+        nb_first = sb.tile([P, HALF], F32, name="nb_first")
+        nb_second = sb.tile([P, HALF], F32, name="nb_second")
+        nc.scalar.activation(nb_first[:], b_sb[:].indirect(half(note_list, 0)), COPY, scale=-1.0)
+        nc.vector.tensor_copy(out=a_second[:], in_=a_sb[:].indirect(half(token_list, 1)))
+        nc.scalar.activation(nb_second[:], b_sb[:].indirect(half(note_list, 1)), COPY, scale=-1.0)
+
+        nc.vector.tensor_tensor(f1[:].indirect(half(tug_list, 0)), a_first[:], nb_first[:], ADD)
+        nc.vector.tensor_tensor(f1[:].indirect(half(tug_list, 1)), a_second[:], nb_second[:], ADD)
+
+        nc.gpsimd.tensor_tensor(a_second[:], a_second[:], nb_second[:], ADD)
+        r_second = a_second
+        nc.gpsimd.tensor_tensor(nb_second[:], a_first[:], nb_first[:], ADD)
+        r_first = nb_second
+
+        for h in range(2):
+            cols = slice(h * BANK, (h + 1) * BANK)
+            nc.vector.scalar_tensor_tensor(
+                out=cc[:, cols], in0=f1[:, cols], scalar=lam_sb[:], in1=c_banks[h][:], op0=MULT, op1=ADD
+            )
+
+        y_second = sb.tile([P, HALF], F32, name="y_second")
+        y_first = sb.tile([P, HALF], F32, name="y_first")
+        cc_first = sb.tile([P, HALF], F32, name="cc_first")
+        nc.vector.tensor_tensor(y_second[:], cc[:].indirect(half(read_list, 1)), r_second[:], SUB)
+        nc.scalar.activation(cc_first[:], cc[:].indirect(half(read_list, 0)), COPY)
+        nc.sync.dma_start(out=out[:, HALF:], in_=y_second[:])
+        nc.vector.tensor_tensor(y_first[:], cc_first[:], r_first[:], SUB)
+        nc.sync.dma_start(out=out[:, :HALF], in_=y_first[:])

@@ -21,7 +21,6 @@ D, COLS, SLOTS, Q = 512, 1024, 512, 128
 BANK = 512
 HALF = SLOTS // 2
 LIST_COLS = SLOTS // 16
-CAST_SPLIT = 48
 
 FLOPS = 2 * Q * D * 3 * COLS
 
@@ -65,29 +64,32 @@ def tile_attend_tugged_three_kernel(tc, query, keys_words, keys_scales, notes_wo
         b_sb = sb.tile([P, COLS], F32, name="b_sb")
         f1 = sb.tile([P, COLS], F32, name="f1")
         cc = sb.tile([P, COLS], F32, name="cc")
+        minus_one = sb.tile([P, HALF], F32, name="minus_one")
 
         for plane in (k_scale, n_scale, u_scale):
             nc.vector.memset(plane[:].bitcast(I32), 0)
+        nc.vector.memset(minus_one[:], -1.0)
         nc.vector.memset(f1[:], 0.0)
 
-        nc.sync.dma_start(token_list[:], offs)
         nc.sync.dma_start(out=q_raw[:], in_=query.rearrange("(p j) q -> p j q", j=PACK))
         load_scale_rows(nc, k_scale, keys_scales)
-        nc.sync.dma_start(note_list[:], offs2)
+        nc.sync.dma_start(token_list[:], offs)
         nc.sync.dma_start(out=k_words[:].bitcast(I32), in_=keys_words[0].bitcast(I32))
         nc.sync.dma_start(
             out=n_words[:].bitcast(I32), in_=notes_words[0].rearrange("p n t -> p (n t)").bitcast(I32)
         )
         load_scale_rows(nc, n_scale, notes_scales)
+        nc.sync.dma_start(note_list[:], offs2)
         nc.sync.dma_start(tug_list[:], offs3)
         load_scale_rows(nc, u_scale, users_scales)
         nc.sync.dma_start(out=u_words[:].bitcast(I32), in_=users_words[0].bitcast(I32))
         nc.sync.dma_start(out=lam_sb[:], in_=lam)
         nc.sync.dma_start(read_list[:], offs4)
 
-        q_src = q_raw[:].rearrange("p j q -> p q j")
-        nc.vector.tensor_copy(out=q_bf[:, :CAST_SPLIT, :], in_=q_src[:, :CAST_SPLIT, :])
-        nc.scalar.activation(q_bf[:, CAST_SPLIT:, :], q_src[:, CAST_SPLIT:, :], COPY)
+        nc.vector.tensor_copy(
+            out=q_bf[:].rearrange("p (c i) j -> p c j i", i=4),
+            in_=q_raw[:].rearrange("p j (c i) -> p c j i", i=4),
+        )
         nc.vector.quantize_mx(
             out=q_codes[:].bitcast(FP8X4), scales=q_scale[:], in_=q_bf[:].rearrange("p q j -> p (q j)")
         )
@@ -111,35 +113,34 @@ def tile_attend_tugged_three_kernel(tc, query, keys_words, keys_scales, notes_wo
         def fp8_scores(name, words, scale, first, width):
             return scores(name, words[:, first : first + width].bitcast(FP8X4), scale, first, width)
 
-        a0 = fp4_scores("a0", k_words, k_scale, 0, BANK)
-        a1 = fp4_scores("a1", k_words, k_scale, BANK, BANK)
-        b0 = fp8_scores("b0", n_words, n_scale, 0, BANK)
-        b1 = fp8_scores("b1", n_words, n_scale, BANK, BANK // 2)
-        b2 = fp8_scores("b2", n_words, n_scale, BANK + BANK // 2, BANK // 2)
+        quarter = BANK // 2
+        pieces = ((0, BANK), (BANK, quarter), (BANK + quarter, quarter))
+        a_banks = [fp4_scores("a%d" % n, k_words, k_scale, first, width) for n, (first, width) in enumerate(pieces)]
+        b_banks = [fp8_scores("b%d" % n, n_words, n_scale, first, width) for n, (first, width) in enumerate(pieces)]
         c_banks = [fp4_scores("c%d" % h, u_words, u_scale, h * BANK, BANK) for h in range(2)]
 
-        nc.vector.tensor_copy(out=a_sb[:, :BANK], in_=a0[:])
-        nc.scalar.activation(a_sb[:, BANK:], a1[:], COPY)
+        def unload(dst, banks):
+            nc.vector.tensor_copy(out=dst[:, :BANK], in_=banks[0][:])
+            nc.scalar.activation(dst[:, BANK : BANK + quarter], banks[1][:], COPY)
+            nc.vector.tensor_copy(out=dst[:, BANK + quarter :], in_=banks[2][:])
+
+        unload(a_sb, a_banks)
         a_first = sb.tile([P, HALF], F32, name="a_first")
         nc.scalar.activation(a_first[:], a_sb[:].indirect(half(token_list, 0)), COPY)
-        nc.vector.tensor_copy(out=b_sb[:, :BANK], in_=b0[:])
-        nc.scalar.activation(b_sb[:, BANK : BANK + BANK // 2], b1[:], COPY)
-        nc.vector.tensor_copy(out=b_sb[:, BANK + BANK // 2 :], in_=b2[:])
+        unload(b_sb, b_banks)
 
         a_second = sb.tile([P, HALF], F32, name="a_second", tag="notes_then_a", align_bytes=64)
-        nb_first = sb.tile([P, HALF], F32, name="nb_first")
-        nb_second = sb.tile([P, HALF], F32, name="nb_second")
-        nc.scalar.activation(nb_first[:], b_sb[:].indirect(half(note_list, 0)), COPY, scale=-1.0)
-        nc.vector.tensor_copy(out=a_second[:], in_=a_sb[:].indirect(half(token_list, 1)))
-        nc.scalar.activation(nb_second[:], b_sb[:].indirect(half(note_list, 1)), COPY, scale=-1.0)
+        neg_r_first = sb.tile([P, HALF], F32, name="neg_r_first")
+        neg_b_second = sb.tile([P, HALF], F32, name="neg_b_second")
+        nc.vector.tensor_tensor(neg_r_first[:], b_sb[:].indirect(half(note_list, 0)), a_first[:], SUB)
+        nc.scalar.activation(a_second[:], a_sb[:].indirect(half(token_list, 1)), COPY)
+        nc.scalar.activation(neg_b_second[:], b_sb[:].indirect(half(note_list, 1)), COPY, scale=-1.0)
 
-        nc.vector.tensor_tensor(f1[:].indirect(half(tug_list, 0)), a_first[:], nb_first[:], ADD)
-        nc.vector.tensor_tensor(f1[:].indirect(half(tug_list, 1)), a_second[:], nb_second[:], ADD)
+        nc.vector.tensor_tensor(f1[:].indirect(half(tug_list, 0)), neg_r_first[:], minus_one[:], MULT)
+        nc.vector.tensor_tensor(f1[:].indirect(half(tug_list, 1)), a_second[:], neg_b_second[:], ADD)
 
-        nc.gpsimd.tensor_tensor(a_second[:], a_second[:], nb_second[:], ADD)
+        nc.gpsimd.tensor_tensor(a_second[:], a_second[:], neg_b_second[:], ADD)
         r_second = a_second
-        nc.gpsimd.tensor_tensor(nb_second[:], a_first[:], nb_first[:], ADD)
-        r_first = nb_second
 
         for h in range(2):
             cols = slice(h * BANK, (h + 1) * BANK)
@@ -147,11 +148,9 @@ def tile_attend_tugged_three_kernel(tc, query, keys_words, keys_scales, notes_wo
                 out=cc[:, cols], in0=f1[:, cols], scalar=lam_sb[:], in1=c_banks[h][:], op0=MULT, op1=ADD
             )
 
-        y_second = sb.tile([P, HALF], F32, name="y_second")
         y_first = sb.tile([P, HALF], F32, name="y_first")
-        cc_first = sb.tile([P, HALF], F32, name="cc_first")
-        nc.vector.tensor_tensor(y_second[:], cc[:].indirect(half(read_list, 1)), r_second[:], SUB)
-        nc.scalar.activation(cc_first[:], cc[:].indirect(half(read_list, 0)), COPY)
-        nc.sync.dma_start(out=out[:, HALF:], in_=y_second[:])
-        nc.vector.tensor_tensor(y_first[:], cc_first[:], r_first[:], SUB)
+        y_second = sb.tile([P, HALF], F32, name="y_second")
+        nc.vector.tensor_tensor(y_first[:], cc[:].indirect(half(read_list, 0)), neg_r_first[:], ADD)
         nc.sync.dma_start(out=out[:, :HALF], in_=y_first[:])
+        nc.vector.tensor_tensor(y_second[:], cc[:].indirect(half(read_list, 1)), r_second[:], SUB)
+        nc.sync.dma_start(out=out[:, HALF:], in_=y_second[:])

@@ -26,10 +26,10 @@ FLOPS = 2 * Q * D * 3 * COLS
 
 
 def load_scale_rows(nc, plane, scales):
-    for quad in range(4):
+    for row in range(4):
         nc.sync.dma_start(
-            out=plane[32 * quad : 32 * quad + 4, :].bitcast(I32),
-            in_=scales[0, 4 * quad : 4 * quad + 4, :].bitcast(I32),
+            out=plane[row:P:32, :].bitcast(I32),
+            in_=scales[0, row:16:4, :].bitcast(I32),
         )
 
 
@@ -54,7 +54,8 @@ def tile_attend_tugged_three_kernel(tc, query, keys_words, keys_scales, notes_wo
         q_codes = sb.tile([P, Q], U32, name="q_codes", align_bytes=64)
         q_scale = sb.tile([P, Q], U8, name="q_scale", align_bytes=64)
         k_words = sb.tile([P, 2 * COLS], U8, name="k_words", align_bytes=64)
-        n_words = sb.tile([P, COLS], U32, name="n_words", tag="notes_then_a", align_bytes=64)
+        n_words_lo = sb.tile([P, BANK], U32, name="n_words_lo", align_bytes=64)
+        n_words_hi = sb.tile([P, BANK], U32, name="n_words_hi", tag="notes_then_a", align_bytes=64)
         u_words = sb.tile([P, 2 * COLS], U8, name="u_words", align_bytes=64)
         k_scale = sb.tile([P, COLS], U8, name="k_scale", align_bytes=64)
         n_scale = sb.tile([P, COLS], U8, name="n_scale", align_bytes=64)
@@ -71,15 +72,15 @@ def tile_attend_tugged_three_kernel(tc, query, keys_words, keys_scales, notes_wo
         nc.vector.memset(minus_one[:], -1.0)
         nc.vector.memset(f1[:], 0.0)
 
+        nc.sync.dma_start(token_list[:], offs)
         nc.sync.dma_start(out=q_raw[:], in_=query.rearrange("(p j) q -> p j q", j=PACK))
         load_scale_rows(nc, k_scale, keys_scales)
-        nc.sync.dma_start(token_list[:], offs)
-        nc.sync.dma_start(out=k_words[:].bitcast(I32), in_=keys_words[0].bitcast(I32))
-        nc.sync.dma_start(
-            out=n_words[:].bitcast(I32), in_=notes_words[0].rearrange("p n t -> p (n t)").bitcast(I32)
-        )
-        load_scale_rows(nc, n_scale, notes_scales)
         nc.sync.dma_start(note_list[:], offs2)
+        nc.sync.dma_start(out=k_words[:].bitcast(I32), in_=keys_words[0].bitcast(I32))
+        notes_i32 = notes_words[0].rearrange("p n t -> p (n t)").bitcast(I32)
+        nc.sync.dma_start(out=n_words_lo[:].bitcast(I32), in_=notes_i32[:, :BANK])
+        load_scale_rows(nc, n_scale, notes_scales)
+        nc.sync.dma_start(out=n_words_hi[:].bitcast(I32), in_=notes_i32[:, BANK:])
         nc.sync.dma_start(tug_list[:], offs3)
         load_scale_rows(nc, u_scale, users_scales)
         nc.sync.dma_start(out=u_words[:].bitcast(I32), in_=users_words[0].bitcast(I32))
@@ -110,13 +111,15 @@ def tile_attend_tugged_three_kernel(tc, query, keys_words, keys_scales, notes_wo
         def fp4_scores(name, words, scale, first, width):
             return scores(name, words[:, 2 * first : 2 * (first + width)].bitcast(FP4X4), scale, first, width)
 
-        def fp8_scores(name, words, scale, first, width):
-            return scores(name, words[:, first : first + width].bitcast(FP8X4), scale, first, width)
+        def note_scores(name, first, width):
+            words = n_words_lo if first < BANK else n_words_hi
+            at = first % BANK
+            return scores(name, words[:, at : at + width].bitcast(FP8X4), n_scale, first, width)
 
         quarter = BANK // 2
         pieces = ((0, BANK), (BANK, quarter), (BANK + quarter, quarter))
         a_banks = [fp4_scores("a%d" % n, k_words, k_scale, first, width) for n, (first, width) in enumerate(pieces)]
-        b_banks = [fp8_scores("b%d" % n, n_words, n_scale, first, width) for n, (first, width) in enumerate(pieces)]
+        b_banks = [note_scores("b%d" % n, first, width) for n, (first, width) in enumerate(pieces)]
         c_banks = [fp4_scores("c%d" % h, u_words, u_scale, h * BANK, BANK) for h in range(2)]
 
         def unload(dst, banks):

from contextlib import ExitStack

import concourse.mybir as mybir

F32 = mybir.dt.float32
BF16 = mybir.dt.bfloat16
I32 = mybir.dt.int32
U32 = mybir.dt.uint32
U16 = mybir.dt.uint16
U8 = mybir.dt.uint8
FP8X4 = mybir.dt.float8_e4m3fn_x4
FP4X4 = mybir.dt.float4_e2m1fn_x4
COPY = mybir.ActivationFunctionType.Copy
ADD = mybir.AluOpType.add
SUB = mybir.AluOpType.subtract
MULT = mybir.AluOpType.mult

P = 128
PACK = 4
D, COLS, SLOTS, Q = 512, 1024, 512, 128
BANK = 512
HALF = SLOTS // 2
LIST_COLS = SLOTS // 16

FLOPS = 2 * Q * D * 3 * COLS


def load_scale_rows(nc, plane, scales):
    for row in range(4):
        nc.sync.dma_start(
            out=plane[row:P:32, :].bitcast(I32),
            in_=scales[0, row:16:4, :].bitcast(I32),
        )


def tile_attend_tugged_three_kernel(tc, query, keys_words, keys_scales, notes_words, notes_scales,
                                     users_words, users_scales, lam, offs, offs2, offs3, offs4, out):
    nc = tc.nc
    with ExitStack() as ctx:
        lists = ctx.enter_context(tc.tile_pool(name="lists", bufs=1))
        sb = ctx.enter_context(tc.tile_pool(name="sb", bufs=1))
        ps = ctx.enter_context(tc.psum_pool(name="ps", bufs=1))

        token_list = lists.tile([P, LIST_COLS], U16, name="token_list")
        note_list = lists.tile([P, LIST_COLS], U16, name="note_list")
        tug_list = lists.tile([P, LIST_COLS], U16, name="tug_list")
        read_list = lists.tile([P, LIST_COLS], U16, name="read_list")

        def half(lst, h):
            return lst[:, h * (LIST_COLS // 2) : (h + 1) * (LIST_COLS // 2)]

        q_raw = sb.tile([P, PACK, Q], F32, name="q_raw")
        q_bf = sb.tile([P, Q, PACK], BF16, name="q_bf", align_bytes=64)
        q_codes = sb.tile([P, Q], U32, name="q_codes", align_bytes=64)
        q_scale = sb.tile([P, Q], U8, name="q_scale", align_bytes=64)
        k_words = sb.tile([P, 2 * COLS], U8, name="k_words", align_bytes=64)
        n_words_lo = sb.tile([P, BANK], U32, name="n_words_lo", align_bytes=64)
        n_words_hi = sb.tile([P, BANK], U32, name="n_words_hi", tag="notes_then_a", align_bytes=64)
        u_words = sb.tile([P, 2 * COLS], U8, name="u_words", align_bytes=64)
        k_scale = sb.tile([P, COLS], U8, name="k_scale", align_bytes=64)
        n_scale = sb.tile([P, COLS], U8, name="n_scale", align_bytes=64)
        u_scale = sb.tile([P, COLS], U8, name="u_scale", align_bytes=64)
        lam_sb = sb.tile([P, 1], F32, name="lam_sb")
        a_sb = sb.tile([P, COLS], F32, name="a_sb")
        b_sb = sb.tile([P, COLS], F32, name="b_sb")
        f1 = sb.tile([P, COLS], F32, name="f1")
        cc = sb.tile([P, COLS], F32, name="cc")
        minus_one = sb.tile([P, HALF], F32, name="minus_one")

        for plane in (k_scale, n_scale, u_scale):
            nc.vector.memset(plane[:].bitcast(I32), 0)
        nc.vector.memset(minus_one[:], -1.0)
        nc.vector.memset(f1[:], 0.0)

        nc.sync.dma_start(token_list[:], offs)
        nc.sync.dma_start(out=q_raw[:], in_=query.rearrange("(p j) q -> p j q", j=PACK))
        load_scale_rows(nc, k_scale, keys_scales)
        nc.sync.dma_start(note_list[:], offs2)
        nc.sync.dma_start(out=k_words[:].bitcast(I32), in_=keys_words[0].bitcast(I32))
        notes_i32 = notes_words[0].rearrange("p n t -> p (n t)").bitcast(I32)
        nc.sync.dma_start(out=n_words_lo[:].bitcast(I32), in_=notes_i32[:, :BANK])
        load_scale_rows(nc, n_scale, notes_scales)
        nc.sync.dma_start(out=n_words_hi[:].bitcast(I32), in_=notes_i32[:, BANK:])
        nc.sync.dma_start(tug_list[:], offs3)
        load_scale_rows(nc, u_scale, users_scales)
        nc.sync.dma_start(out=u_words[:].bitcast(I32), in_=users_words[0].bitcast(I32))
        nc.sync.dma_start(out=lam_sb[:], in_=lam)
        nc.sync.dma_start(read_list[:], offs4)

        nc.vector.tensor_copy(
            out=q_bf[:].rearrange("p (c i) j -> p c j i", i=4),
            in_=q_raw[:].rearrange("p j (c i) -> p c j i", i=4),
        )
        nc.vector.quantize_mx(
            out=q_codes[:].bitcast(FP8X4), scales=q_scale[:], in_=q_bf[:].rearrange("p q j -> p (q j)")
        )

        def scores(name, words, scale, first, width):
            bank = ps.tile([Q, width], F32, name=name)
            nc.tensor.matmul_mx(
                out=bank[:],
                lhsT=q_codes[:].bitcast(FP8X4),
                lhsT_scale=q_scale[:],
                rhs=words,
                rhs_scale=scale[:, first : first + width],
                start=True,
                stop=True,
            )
            return bank

        def fp4_scores(name, words, scale, first, width):
            return scores(name, words[:, 2 * first : 2 * (first + width)].bitcast(FP4X4), scale, first, width)

        def note_scores(name, first, width):
            words = n_words_lo if first < BANK else n_words_hi
            at = first % BANK
            return scores(name, words[:, at : at + width].bitcast(FP8X4), n_scale, first, width)

        quarter = BANK // 2
        pieces = ((0, BANK), (BANK, quarter), (BANK + quarter, quarter))
        a_banks = [fp4_scores("a%d" % n, k_words, k_scale, first, width) for n, (first, width) in enumerate(pieces)]
        b_banks = [note_scores("b%d" % n, first, width) for n, (first, width) in enumerate(pieces)]
        c_banks = [fp4_scores("c%d" % h, u_words, u_scale, h * BANK, BANK) for h in range(2)]

        def unload(dst, banks):
            nc.vector.tensor_copy(out=dst[:, :BANK], in_=banks[0][:])
            nc.scalar.activation(dst[:, BANK : BANK + quarter], banks[1][:], COPY)
            nc.vector.tensor_copy(out=dst[:, BANK + quarter :], in_=banks[2][:])

        unload(a_sb, a_banks)
        a_first = sb.tile([P, HALF], F32, name="a_first")
        nc.scalar.activation(a_first[:], a_sb[:].indirect(half(token_list, 0)), COPY)
        unload(b_sb, b_banks)

        a_second = sb.tile([P, HALF], F32, name="a_second", tag="notes_then_a", align_bytes=64)
        neg_r_first = sb.tile([P, HALF], F32, name="neg_r_first")
        neg_b_second = sb.tile([P, HALF], F32, name="neg_b_second")
        nc.vector.tensor_tensor(neg_r_first[:], b_sb[:].indirect(half(note_list, 0)), a_first[:], SUB)
        nc.scalar.activation(a_second[:], a_sb[:].indirect(half(token_list, 1)), COPY)
        nc.scalar.activation(neg_b_second[:], b_sb[:].indirect(half(note_list, 1)), COPY, scale=-1.0)

        nc.vector.tensor_tensor(f1[:].indirect(half(tug_list, 0)), neg_r_first[:], minus_one[:], MULT)
        nc.vector.tensor_tensor(f1[:].indirect(half(tug_list, 1)), a_second[:], neg_b_second[:], ADD)

        nc.gpsimd.tensor_tensor(a_second[:], a_second[:], neg_b_second[:], ADD)
        r_second = a_second

        for h in range(2):
            cols = slice(h * BANK, (h + 1) * BANK)
            nc.vector.scalar_tensor_tensor(
                out=cc[:, cols], in0=f1[:, cols], scalar=lam_sb[:], in1=c_banks[h][:], op0=MULT, op1=ADD
            )

        y_first = sb.tile([P, HALF], F32, name="y_first")
        y_second = sb.tile([P, HALF], F32, name="y_second")
        nc.vector.tensor_tensor(y_first[:], cc[:].indirect(half(read_list, 0)), neg_r_first[:], ADD)
        nc.sync.dma_start(out=out[:, :HALF], in_=y_first[:])
        nc.vector.tensor_tensor(y_second[:], cc[:].indirect(half(read_list, 1)), r_second[:], SUB)
        nc.sync.dma_start(out=out[:, HALF:], in_=y_second[:])
